import numpy as np
import ml_dtypes


def mxq(x, axis, fmt="e4m3"):
    dtype, down = {"e4m3": (ml_dtypes.float8_e4m3fn, 7), "e5m2": (ml_dtypes.float8_e5m2, 14)}[fmt]
    v = np.moveaxis(np.asarray(x, np.float32).astype(ml_dtypes.bfloat16).astype(np.float64), axis, -1)
    blocks = v.reshape(v.shape[:-1] + (-1, 32))
    amax = np.abs(blocks).max(-1, keepdims=True)
    byte = np.maximum(np.where(amax > 0, np.frexp(amax)[1] - 1 + 127, 0) - down, 1)
    scale = np.exp2(byte - 127.0)
    codes = (blocks / scale).astype(np.float32).astype(dtype).astype(np.float64)
    return np.moveaxis((codes * scale).reshape(v.shape), -1, axis)


WIDE = False


def mx_kscale(k):
    if not WIDE:
        return np.ones(k)
    levels = np.array([10, -10, 5, -5, 0])
    if k % 512:
        return np.exp2(np.random.permutation(np.resize(levels, k // 32))).repeat(32)
    a = np.empty((k // 512, 16))
    for p in range(k // 512):
        a[p, :8] = np.random.permutation(np.resize(levels, 8))
        for g in range(8):
            far = levels[np.abs(levels - a[p, g]) >= 10]
            a[p, g + 8] = far[np.random.randint(len(far))]
    return np.exp2(a.ravel()).repeat(32)


def f64(x):
    return np.asarray(x).astype(np.float64)


def striped8(idx):
    return np.asarray(idx).reshape(8, -1, 16).transpose(0, 2, 1).reshape(128, -1).astype(np.uint16)


def unstriped8(offs):
    return offs.reshape(8, 16, -1).transpose(0, 2, 1).reshape(8, -1).astype(np.int64)


def pick8(x, idx, run):
    r = np.arange(len(x))
    return x[r[:, None], idx[r % (8 * run) // run]]


E2M1 = np.array([0.0, 0.5, 1.0, 1.5, 2.0, 3.0, 4.0, 6.0, -0.0, -0.5, -1.0, -1.5, -2.0, -3.0, -4.0, -6.0])


def pack_weight(w, fmt):
    k, n = w.shape
    w = f64(np.asarray(w, np.float32).astype(ml_dtypes.bfloat16)).reshape(k // 32, 32, n)
    amax = np.abs(w).max(1)
    if fmt == "e4m3":
        byte = np.frexp(amax)[1] - 1 + 127 - 7
    else:
        mant, ex = np.frexp(amax / 6.0)
        byte = np.where(mant > 0.5, ex, ex - 1) + 127
    byte = np.clip(np.where(amax > 0, byte, 1), 1, 254)
    scaled = (w * np.exp2(127.0 - byte)[:, None, :]).reshape(k, n).astype(np.float32)
    by_word = np.ascontiguousarray(scaled.reshape(k // 512, 128, 4, n).transpose(0, 1, 3, 2))
    if fmt == "e4m3":
        words = by_word.astype(ml_dtypes.float8_e4m3fn).view(np.uint8)
    else:
        c = by_word.astype(ml_dtypes.float4_e2m1fn).view(np.uint8) & 0xF
        words = (c[..., 0::2] | (c[..., 1::2] << 4)).reshape(k // 512, 128, 2 * n)
    return np.ascontiguousarray(words), np.ascontiguousarray(byte.astype(np.uint8).reshape(k // 512, 16, n))


def unpack_weight(words, scales, fmt):
    g, _, n = scales.shape
    words = np.ascontiguousarray(words).reshape(g, 128, n, -1)
    if fmt == "e4m3":
        vals = words.view(ml_dtypes.float8_e4m3fn).astype(np.float64)
    else:
        nib = np.empty((g, 128, n, 4), np.uint8)
        nib[..., 0::2] = words & 0xF
        nib[..., 1::2] = words >> 4
        vals = E2M1[nib]
    vals = vals * np.repeat(np.exp2(scales.astype(np.float64) - 127.0), 8, axis=1)[..., None]
    return vals.transpose(0, 1, 3, 2).reshape(g * 512, n)


D, T, I, Q = 512, 1024, 512, 128


def setup_inputs():
    n = np.random.standard_normal
    idx = np.stack([np.random.permutation(T)[:I] for _ in range(8)])
    idx2 = np.stack([np.random.permutation(T)[:I] for _ in range(8)])
    idx3 = np.stack([np.random.permutation(T)[:I] for _ in range(8)])
    idx4 = np.stack([np.random.permutation(T)[:I] for _ in range(8)])
    fd = mx_kscale(D)
    keysp = pack_weight(n((D, T)) / fd[:, None], "e4m3")
    return {
        "query": (n((D, Q)) * 1.2 / np.sqrt(D) * fd[:, None]).astype(np.float32),
        "keys_words": keysp[0],
        "keys_scales": keysp[1],
        "lam": (np.random.uniform(0.8, 1.8, (Q, 1))).astype(np.float32),
        "old": (1.0 * n((Q, T))).astype(np.float32),
        "share2": (np.random.uniform(0.4, 1.2, (Q, 1))).astype(np.float32),
        "offs": striped8(idx),
        "offs2": striped8(idx2),
        "offs3": striped8(idx3),
        "offs4": striped8(idx4),
    }


def reference(query, keys_words, keys_scales, lam, old, share2, offs, offs2, offs3, offs4):
    idx = unstriped8(offs)
    idx2 = unstriped8(offs2)
    idx3 = unstriped8(offs3)
    idx4 = unstriped8(offs4)
    keysu = unpack_weight(keys_words, keys_scales, "e4m3")
    queryq = mxq(f64(query), 0, "e4m3")
    a = queryq.T @ keysu
    lo2 = np.minimum(pick8(a, idx, 16), pick8(a, idx2, 16))
    hi2 = np.maximum(pick8(a, idx, 16), pick8(a, idx2, 16))
    s = np.maximum(lo2, np.minimum(hi2, pick8(a, idx3, 16))) * f64(lam)
    w = np.maximum(s, 0.0)
    f1 = np.zeros((Q, T))
    f1[np.arange(Q)[:, None], idx[np.arange(Q) % 128 // 16]] = w
    f2 = np.zeros((Q, T))
    f2[np.arange(Q)[:, None], idx4[np.arange(Q) % 128 // 16]] = w
    y = f64(old) + f1 + f2 * f64(share2)
    return y

@@ -1,0 +1,169 @@
+from contextlib import ExitStack
+
+import concourse.mybir as mybir
+from concourse.masks import make_identity
+
+D, T, I, Q = 512, 1024, 512, 128
+FLOPS = 2 * D * T * Q
+
+F32 = mybir.dt.float32
+BF16 = mybir.dt.bfloat16
+I32 = mybir.dt.int32
+U32 = mybir.dt.uint32
+U16 = mybir.dt.uint16
+U8 = mybir.dt.uint8
+FP8X4 = mybir.dt.float8_e4m3fn_x4
+ALU = mybir.AluOpType
+COPY = mybir.ActivationFunctionType.Copy
+
+P = 128
+PACK = 4
+N_MM = 256
+HALF = I // 2
+PIECE = 128
+REST = I - PIECE
+BANK = 256
+STORE = 256
+BIG = 2.0 ** 127
+
+
+def tile_attend_middle_lean_twiceput_heads_kernel(
+    tc, query, keys_words, keys_scales, lam, old, share2, offs, offs2, offs3, offs4, out
+):
+    nc = tc.nc
+    with ExitStack() as ctx:
+        sb = ctx.enter_context(tc.tile_pool(name="sb", bufs=1))
+        ps = ctx.enter_context(tc.psum_pool(name="ps", bufs=1))
+
+        lists = [sb.tile([P, I // 16], U16, name="list%d" % n) for n in range(4)]
+        k_scales = sb.tile([P, T], U8, align_bytes=64)
+        k_words = sb.tile([P, T], U32, align_bytes=64)
+        q_raw = sb.tile([P, PACK, Q], F32, align_bytes=64)
+        lam_col = sb.tile([P, 1], F32)
+        share_col = sb.tile([P, 1], F32)
+        old_sb = sb.tile([P, T], F32)
+
+        nc.gpsimd.memset(k_scales[:].bitcast(I32), 0)
+        nc.gpsimd.dma_start(lam_col[:], lam)
+        nc.gpsimd.dma_start(share_col[:], share2)
+        nc.sync.dma_start(q_raw[:], query.rearrange("(p j) q -> p j q", j=PACK))
+        for quad in range(4):
+            nc.sync.dma_start(
+                k_scales[32 * quad : 32 * quad + 4, :].bitcast(I32),
+                keys_scales[0][4 * quad : 4 * quad + 4, :].bitcast(I32),
+            )
+        nc.sync.dma_start(k_words[:].bitcast(I32), keys_words[0].rearrange("p n t -> p (n t)").bitcast(I32))
+        nc.sync.dma_start(lists[0][:], offs)
+        nc.sync.dma_start(lists[1][:], offs2)
+        nc.sync.dma_start(lists[2][:], offs3)
+        nc.sync.dma_start(lists[3][:], offs4)
+        nc.sync.dma_start(old_sb[:], old)
+
+        put1 = sb.tile([P, T], F32)
+        put2 = sb.tile([P, T], F32)
+        nc.vector.memset(put1[:], 0.0)
+        nc.vector.memset(put2[:], 0.0)
+        ones = sb.tile([P, REST], F32)
+        nc.gpsimd.memset(ones[:], 1.0)
+        ident = sb.tile([P, P], F32)
+        make_identity(nc, ident[:])
+
+        q_bf = sb.tile([P, Q, PACK], BF16, align_bytes=64)
+        nc.vector.tensor_copy(
+            q_bf[:].rearrange("p (c i) j -> p c j i", i=4), q_raw[:].rearrange("p j (c i) -> p c j i", i=4)
+        )
+        q_codes = sb.tile([P, Q], U32, align_bytes=64)
+        q_scales = sb.tile([P, Q], U8, align_bytes=64)
+        nc.vector.quantize_mx(q_codes[:].bitcast(FP8X4), q_scales[:], q_bf[:].rearrange("p q j -> p (q j)"))
+
+        top = sb.tile([P, 1], F32)
+        bottom = sb.tile([P, 1], F32)
+        nc.gpsimd.tensor_scalar(top[:], lam_col[:], 0.0, BIG, ALU.is_ge, ALU.mult)
+        nc.gpsimd.tensor_scalar(bottom[:], lam_col[:], 0.0, -BIG, ALU.is_lt, ALU.mult)
+        lam_row = sb.tile([P, HALF], F32)
+        nc.gpsimd.tensor_scalar(lam_row[:], ones[:, :HALF], lam_col[:], 0.0, ALU.mult, ALU.add)
+        both_col = sb.tile([P, 1], F32)
+        nc.gpsimd.tensor_tensor(both_col[:], lam_col[:], share_col[:], ALU.mult)
+        both_row = sb.tile([P, REST], F32)
+        nc.gpsimd.tensor_scalar(both_row[:], ones[:], both_col[:], 0.0, ALU.mult, ALU.add)
+
+        scores = sb.tile([P, T], F32)
+        for n in range(T // N_MM):
+            cols = slice(n * N_MM, (n + 1) * N_MM)
+            acc = ps.tile([P, N_MM], F32, name="acc%d" % n, tag="bank%d" % n)
+            nc.tensor.matmul_mx(
+                acc[:], q_codes[:].bitcast(FP8X4), q_scales[:], k_words[:, cols].bitcast(FP8X4), k_scales[:, cols],
+                start=True, stop=True,
+            )
+            if n % 2 == 0:
+                nc.vector.tensor_copy(scores[:, cols], acc[:])
+            else:
+                nc.scalar.copy(scores[:, cols], acc[:])
+
+        turned = [ps.tile([P, BANK], F32, name="turned%d" % b, tag="bank%d" % b) for b in range(T // BANK)]
+        for b in range(T // BANK):
+            for j in range(BANK // P):
+                nc.tensor.matmul(
+                    turned[b][:, j * P : (j + 1) * P], old_sb[:, b * BANK + j * P : b * BANK + (j + 1) * P], ident[:],
+                    start=(j == 0), stop=False, is_transpose=True,
+                )
+
+        clamped = sb.tile([P, I], F32)
+
+        def put(window, offsets, row, start, stop):
+            nc.vector.tensor_tensor(
+                window[:].indirect(offsets[:, start // 16 : stop // 16]), clamped[:, start:stop], row[:, : stop - start],
+                ALU.mult,
+            )
+
+        def look_up(h):
+            entries = slice(h * HALF // 16, (h + 1) * HALF // 16)
+            first = sb.tile([P, HALF], F32, name="first%d" % h)
+            second = sb.tile([P, HALF], F32, name="second%d" % h)
+            third = sb.tile([P, HALF], F32, name="third%d" % h)
+            nc.scalar.activation(first[:], scores[:].indirect(lists[0][:, entries]), COPY)
+            if h == 0:
+                nc.vector.tensor_copy(second[:], scores[:].indirect(lists[1][:, entries]))
+            else:
+                nc.scalar.activation(second[:], scores[:].indirect(lists[1][:, entries]), COPY)
+            nc.scalar.activation(third[:], scores[:].indirect(lists[2][:, entries]), COPY)
+            pair = sb.tile([P, 2, HALF], F32, name="pair")
+            nc.vector.tensor_tensor(pair[:, 0, :], first[:], second[:], ALU.max)
+            nc.vector.scalar_tensor_tensor(pair[:, 1, :], first[:], top[:], second[:], ALU.min, ALU.min)
+            return pair, third
+
+        pair, third = look_up(0)
+        mid = sb.tile([P, I], F32)
+        pieces = [slice(c, c + PIECE) for c in range(0, HALF, PIECE)]
+        for c in pieces:
+            nc.vector.scalar_tensor_tensor(mid[:, c], pair[:, 0, c], top[:], third[:, c], ALU.min, ALU.min)
+        for c in pieces:
+            nc.vector.scalar_tensor_tensor(clamped[:, c], pair[:, 1, c], bottom[:], mid[:, c], ALU.max, ALU.max)
+        put(put1, lists[0], lam_row, 0, PIECE)
+        pair, third = look_up(1)
+        nc.vector.scalar_tensor_tensor(mid[:, HALF:], pair[:, 0, :], top[:], third[:], ALU.min, ALU.min)
+        put(put1, lists[0], lam_row, PIECE, HALF)
+        nc.vector.scalar_tensor_tensor(clamped[:, HALF:], pair[:, 1, :], bottom[:], mid[:, HALF:], ALU.max, ALU.max)
+        put(put2, lists[3], both_row, 0, PIECE)
+        put(put1, lists[0], lam_row, HALF, I)
+        put(put2, lists[3], both_row, PIECE, I)
+
+        partial = [ps.tile([P, BANK], F32, name="partial%d" % b) for b in range(T // BANK)]
+        for b in range(T // BANK):
+            for j in range(BANK // P):
+                nc.tensor.matmul(
+                    turned[b][:, j * P : (j + 1) * P], put1[:, b * BANK + j * P : b * BANK + (j + 1) * P], ident[:],
+                    start=False, stop=(j == BANK // P - 1), is_transpose=True,
+                )
+        for b in range(T // BANK):
+            turned_sb = sb.tile([P, BANK], F32, name="turned_sb%d" % b)
+            nc.scalar.copy(turned_sb[:], turned[b][:])
+            for j in range(BANK // P):
+                nc.tensor.transpose(partial[b][:, j * P : (j + 1) * P], turned_sb[:, j * P : (j + 1) * P], ident[:])
+
+        for s in range(T // STORE):
+            cols = slice(s * STORE, (s + 1) * STORE)
+            b, c0 = divmod(s * STORE, BANK)
+            total = sb.tile([P, STORE], F32, name="total%d" % s)
+            nc.vector.tensor_tensor(total[:], partial[b][:, c0 : c0 + STORE], put2[:, cols], ALU.add)
+            (nc.sync if s % 2 == 0 else nc.scalar).dma_start(out[:, cols], total[:])

@@ -37,25 +37,27 @@ def tile_attend_middle_lean_twiceput_heads_kernel(
 
         lists = [sb.tile([P, I // 16], U16, name="list%d" % n) for n in range(4)]
         k_scales = sb.tile([P, T], U8, align_bytes=64)
-        k_words = sb.tile([P, T], U32, align_bytes=64)
+        k_words = [sb.tile([P, T // 2], U32, align_bytes=64, name="k_words%d" % b) for b in range(2)]
         q_raw = sb.tile([P, PACK, Q], F32, align_bytes=64)
         lam_col = sb.tile([P, 1], F32)
         share_col = sb.tile([P, 1], F32)
         old_sb = sb.tile([P, T], F32)
 
-        nc.gpsimd.memset(k_scales[:].bitcast(I32), 0)
-        nc.gpsimd.dma_start(lam_col[:], lam)
-        nc.gpsimd.dma_start(share_col[:], share2)
+        nc.vector.memset(k_scales[:].bitcast(I32), 0)
+        words = keys_words[0].rearrange("p n t -> p (n t)").bitcast(I32)
         nc.sync.dma_start(q_raw[:], query.rearrange("(p j) q -> p j q", j=PACK))
+        nc.sync.dma_start(k_words[0][:].bitcast(I32), words[:, : T // 2])
         for quad in range(4):
             nc.sync.dma_start(
                 k_scales[32 * quad : 32 * quad + 4, :].bitcast(I32),
                 keys_scales[0][4 * quad : 4 * quad + 4, :].bitcast(I32),
             )
-        nc.sync.dma_start(k_words[:].bitcast(I32), keys_words[0].rearrange("p n t -> p (n t)").bitcast(I32))
+        nc.sync.dma_start(k_words[1][:].bitcast(I32), words[:, T // 2 :])
+        nc.sync.dma_start(lam_col[:], lam)
         nc.sync.dma_start(lists[0][:], offs)
         nc.sync.dma_start(lists[1][:], offs2)
         nc.sync.dma_start(lists[2][:], offs3)
+        nc.sync.dma_start(share_col[:], share2)
         nc.sync.dma_start(lists[3][:], offs4)
         nc.sync.dma_start(old_sb[:], old)
 
@@ -63,36 +65,35 @@ def tile_attend_middle_lean_twiceput_heads_kernel(
         put2 = sb.tile([P, T], F32)
         nc.vector.memset(put1[:], 0.0)
         nc.vector.memset(put2[:], 0.0)
-        ones = sb.tile([P, REST], F32)
-        nc.gpsimd.memset(ones[:], 1.0)
         ident = sb.tile([P, P], F32)
         make_identity(nc, ident[:])
 
-        q_bf = sb.tile([P, Q, PACK], BF16, align_bytes=64)
-        nc.vector.tensor_copy(
-            q_bf[:].rearrange("p (c i) j -> p c j i", i=4), q_raw[:].rearrange("p j (c i) -> p c j i", i=4)
-        )
         q_codes = sb.tile([P, Q], U32, align_bytes=64)
         q_scales = sb.tile([P, Q], U8, align_bytes=64)
-        nc.vector.quantize_mx(q_codes[:].bitcast(FP8X4), q_scales[:], q_bf[:].rearrange("p q j -> p (q j)"))
+        q_halves = [slice(c, c + Q // 2) for c in range(0, Q, Q // 2)]
+        q_bf = [sb.tile([P, Q // 2, PACK], BF16, align_bytes=64, name="q_bf%d" % h) for h in range(2)]
+        for h, c in enumerate(q_halves):
+            nc.vector.tensor_copy(
+                q_bf[h][:].rearrange("p (c i) j -> p c j i", i=4), q_raw[:, :, c].rearrange("p j (c i) -> p c j i", i=4)
+            )
+        for h, c in enumerate(q_halves):
+            nc.vector.quantize_mx(
+                q_codes[:, c].bitcast(FP8X4), q_scales[:, c], q_bf[h][:].rearrange("p q j -> p (q j)")
+            )
 
         top = sb.tile([P, 1], F32)
         bottom = sb.tile([P, 1], F32)
         nc.gpsimd.tensor_scalar(top[:], lam_col[:], 0.0, BIG, ALU.is_ge, ALU.mult)
         nc.gpsimd.tensor_scalar(bottom[:], lam_col[:], 0.0, -BIG, ALU.is_lt, ALU.mult)
         lam_row = sb.tile([P, HALF], F32)
-        nc.gpsimd.tensor_scalar(lam_row[:], ones[:, :HALF], lam_col[:], 0.0, ALU.mult, ALU.add)
-        both_col = sb.tile([P, 1], F32)
-        nc.gpsimd.tensor_tensor(both_col[:], lam_col[:], share_col[:], ALU.mult)
-        both_row = sb.tile([P, REST], F32)
-        nc.gpsimd.tensor_scalar(both_row[:], ones[:], both_col[:], 0.0, ALU.mult, ALU.add)
+        nc.scalar.activation(lam_row[:], lam_col[:].to_broadcast([P, HALF]), COPY)
 
         scores = sb.tile([P, T], F32)
         for n in range(T // N_MM):
             cols = slice(n * N_MM, (n + 1) * N_MM)
             acc = ps.tile([P, N_MM], F32, name="acc%d" % n, tag="bank%d" % n)
             nc.tensor.matmul_mx(
-                acc[:], q_codes[:].bitcast(FP8X4), q_scales[:], k_words[:, cols].bitcast(FP8X4), k_scales[:, cols],
+                acc[:], q_codes[:].bitcast(FP8X4), q_scales[:], k_words[n // 2][:, (n % 2) * N_MM : (n % 2 + 1) * N_MM].bitcast(FP8X4), k_scales[:, cols],
                 start=True, stop=True,
             )
             if n % 2 == 0:
@@ -120,7 +121,7 @@ def tile_attend_middle_lean_twiceput_heads_kernel(
             entries = slice(h * HALF // 16, (h + 1) * HALF // 16)
             first = sb.tile([P, HALF], F32, name="first%d" % h)
             second = sb.tile([P, HALF], F32, name="second%d" % h)
-            third = sb.tile([P, HALF], F32, name="third%d" % h)
+            third = sb.tile([P, HALF], F32, name="third%d" % h, tag="third%d" % h)
             nc.scalar.activation(first[:], scores[:].indirect(lists[0][:, entries]), COPY)
             if h == 0:
                 nc.vector.tensor_copy(second[:], scores[:].indirect(lists[1][:, entries]))
@@ -142,6 +143,8 @@ def tile_attend_middle_lean_twiceput_heads_kernel(
         put(put1, lists[0], lam_row, 0, PIECE)
         pair, third = look_up(1)
         nc.vector.scalar_tensor_tensor(mid[:, HALF:], pair[:, 0, :], top[:], third[:], ALU.min, ALU.min)
+        both_row = sb.tile([P, REST], F32, tag="third0")
+        nc.scalar.activation(both_row[:], lam_col[:].to_broadcast([P, REST]), COPY, scale=share_col[:])
         put(put1, lists[0], lam_row, PIECE, HALF)
         nc.vector.scalar_tensor_tensor(clamped[:, HALF:], pair[:, 1, :], bottom[:], mid[:, HALF:], ALU.max, ALU.max)
         put(put2, lists[3], both_row, 0, PIECE)

@@ -18,10 +18,9 @@ COPY = mybir.ActivationFunctionType.Copy
 
 P = 128
 PACK = 4
-N_MM = 256
+WIDTHS = (256, 256, 256, 128, 128)
 HALF = I // 2
 PIECE = 128
-REST = I - PIECE
 BANK = 256
 STORE = 256
 BIG = 2.0 ** 127
@@ -61,17 +60,16 @@ def tile_attend_middle_lean_twiceput_heads_kernel(
         nc.sync.dma_start(lists[3][:], offs4)
         nc.sync.dma_start(old_sb[:], old)
 
-        put1 = sb.tile([P, T], F32)
-        put2 = sb.tile([P, T], F32)
-        nc.vector.memset(put1[:], 0.0)
-        nc.vector.memset(put2[:], 0.0)
+        put1 = [sb.tile([P, T], F32, name="put1_%d" % n) for n in range(2)]
+        for window in put1:
+            nc.vector.memset(window[:], 0.0)
         ident = sb.tile([P, P], F32)
         make_identity(nc, ident[:])
 
         q_codes = sb.tile([P, Q], U32, align_bytes=64)
         q_scales = sb.tile([P, Q], U8, align_bytes=64)
         q_halves = [slice(c, c + Q // 2) for c in range(0, Q, Q // 2)]
-        q_bf = [sb.tile([P, Q // 2, PACK], BF16, align_bytes=64, name="q_bf%d" % h) for h in range(2)]
+        q_bf = [sb.tile([P, Q // 2, PACK], BF16, align_bytes=64, name="q_bf%d" % h, tag="q_bf%d" % h) for h in range(2)]
         for h, c in enumerate(q_halves):
             nc.vector.tensor_copy(
                 q_bf[h][:].rearrange("p (c i) j -> p c j i", i=4), q_raw[:, :, c].rearrange("p j (c i) -> p c j i", i=4)
@@ -81,25 +79,31 @@ def tile_attend_middle_lean_twiceput_heads_kernel(
                 q_codes[:, c].bitcast(FP8X4), q_scales[:, c], q_bf[h][:].rearrange("p q j -> p (q j)")
             )
 
+        put2 = sb.tile([P, T], F32, align_bytes=64, tag="q_bf1")
+        nc.gpsimd.memset(put2[:], 0.0)
+
         top = sb.tile([P, 1], F32)
         bottom = sb.tile([P, 1], F32)
         nc.gpsimd.tensor_scalar(top[:], lam_col[:], 0.0, BIG, ALU.is_ge, ALU.mult)
         nc.gpsimd.tensor_scalar(bottom[:], lam_col[:], 0.0, -BIG, ALU.is_lt, ALU.mult)
-        lam_row = sb.tile([P, HALF], F32)
-        nc.scalar.activation(lam_row[:], lam_col[:].to_broadcast([P, HALF]), COPY)
+        lam_row = sb.tile([P, PIECE], F32)
+        nc.scalar.activation(lam_row[:], lam_col[:].to_broadcast([P, PIECE]), COPY)
 
         scores = sb.tile([P, T], F32)
-        for n in range(T // N_MM):
-            cols = slice(n * N_MM, (n + 1) * N_MM)
-            acc = ps.tile([P, N_MM], F32, name="acc%d" % n, tag="bank%d" % n)
+        start = 0
+        for n, width in enumerate(WIDTHS):
+            cols = slice(start, start + width)
+            half, c0 = divmod(start, T // 2)
+            acc = ps.tile([P, width], F32, name="acc%d" % n, tag="bank%d" % n)
             nc.tensor.matmul_mx(
-                acc[:], q_codes[:].bitcast(FP8X4), q_scales[:], k_words[n // 2][:, (n % 2) * N_MM : (n % 2 + 1) * N_MM].bitcast(FP8X4), k_scales[:, cols],
-                start=True, stop=True,
+                acc[:], q_codes[:].bitcast(FP8X4), q_scales[:], k_words[half][:, c0 : c0 + width].bitcast(FP8X4),
+                k_scales[:, cols], start=True, stop=True,
             )
             if n % 2 == 0:
-                nc.vector.tensor_copy(scores[:, cols], acc[:])
-            else:
                 nc.scalar.copy(scores[:, cols], acc[:])
+            else:
+                nc.vector.tensor_copy(scores[:, cols], acc[:])
+            start = start + width
 
         turned = [ps.tile([P, BANK], F32, name="turned%d" % b, tag="bank%d" % b) for b in range(T // BANK)]
         for b in range(T // BANK):
@@ -133,31 +137,35 @@ def tile_attend_middle_lean_twiceput_heads_kernel(
             nc.vector.scalar_tensor_tensor(pair[:, 1, :], first[:], top[:], second[:], ALU.min, ALU.min)
             return pair, third
 
-        pair, third = look_up(0)
         mid = sb.tile([P, I], F32)
-        pieces = [slice(c, c + PIECE) for c in range(0, HALF, PIECE)]
-        for c in pieces:
-            nc.vector.scalar_tensor_tensor(mid[:, c], pair[:, 0, c], top[:], third[:, c], ALU.min, ALU.min)
-        for c in pieces:
-            nc.vector.scalar_tensor_tensor(clamped[:, c], pair[:, 1, c], bottom[:], mid[:, c], ALU.max, ALU.max)
-        put(put1, lists[0], lam_row, 0, PIECE)
-        pair, third = look_up(1)
-        nc.vector.scalar_tensor_tensor(mid[:, HALF:], pair[:, 0, :], top[:], third[:], ALU.min, ALU.min)
-        both_row = sb.tile([P, REST], F32, tag="third0")
-        nc.scalar.activation(both_row[:], lam_col[:].to_broadcast([P, REST]), COPY, scale=share_col[:])
-        put(put1, lists[0], lam_row, PIECE, HALF)
-        nc.vector.scalar_tensor_tensor(clamped[:, HALF:], pair[:, 1, :], bottom[:], mid[:, HALF:], ALU.max, ALU.max)
-        put(put2, lists[3], both_row, 0, PIECE)
-        put(put1, lists[0], lam_row, HALF, I)
-        put(put2, lists[3], both_row, PIECE, I)
 
-        partial = [ps.tile([P, BANK], F32, name="partial%d" % b) for b in range(T // BANK)]
-        for b in range(T // BANK):
-            for j in range(BANK // P):
-                nc.tensor.matmul(
-                    turned[b][:, j * P : (j + 1) * P], put1[:, b * BANK + j * P : b * BANK + (j + 1) * P], ident[:],
-                    start=False, stop=(j == BANK // P - 1), is_transpose=True,
-                )
+        def median(h):
+            pair, third = look_up(h)
+            pieces = [slice(c, c + PIECE) for c in range(0, HALF, PIECE)]
+            slots = [slice(h * HALF + c.start, h * HALF + c.stop) for c in pieces]
+            for c, d in zip(pieces, slots):
+                nc.vector.scalar_tensor_tensor(mid[:, d], pair[:, 0, c], top[:], third[:, c], ALU.min, ALU.min)
+            for c, d in zip(pieces, slots):
+                nc.vector.scalar_tensor_tensor(clamped[:, d], pair[:, 1, c], bottom[:], mid[:, d], ALU.max, ALU.max)
+
+        median(0)
+        put(put1[0], lists[0], lam_row, 0, PIECE)
+        put(put1[1], lists[0], lam_row, PIECE, HALF)
+        median(1)
+        both_row = sb.tile([P, I], F32, tag="third0")
+        nc.scalar.activation(both_row[:], lam_col[:].to_broadcast([P, I]), COPY, scale=share_col[:])
+        put(put1[0], lists[0], lam_row, HALF, HALF + PIECE)
+        put(put1[1], lists[0], lam_row, HALF + PIECE, I)
+        put(put2, lists[3], both_row, 0, I)
+
+        partial = [ps.tile([P, BANK], F32, name="partial%d" % b, tag="bank%d" % (4 + b)) for b in range(T // BANK)]
+        for n, window in enumerate(put1):
+            for b in range(T // BANK):
+                for j in range(BANK // P):
+                    nc.tensor.matmul(
+                        turned[b][:, j * P : (j + 1) * P], window[:, b * BANK + j * P : b * BANK + (j + 1) * P],
+                        ident[:], start=False, stop=(n == 1 and j == BANK // P - 1), is_transpose=True,
+                    )
         for b in range(T // BANK):
             turned_sb = sb.tile([P, BANK], F32, name="turned_sb%d" % b)
             nc.scalar.copy(turned_sb[:], turned[b][:])

@@ -152,11 +152,15 @@ def tile_attend_middle_lean_twiceput_heads_kernel(
         put(put1[0], lists[0], lam_row, 0, PIECE)
         put(put1[1], lists[0], lam_row, PIECE, HALF)
         median(1)
-        both_row = sb.tile([P, I], F32, tag="third0")
-        nc.scalar.activation(both_row[:], lam_col[:].to_broadcast([P, I]), COPY, scale=share_col[:])
+        both_col = sb.tile([P, 1], F32)
+        nc.gpsimd.tensor_tensor(both_col[:], lam_col[:], share_col[:], ALU.mult)
+        shared = sb.tile([P, I], F32)
+        for h in range(2):
+            slots = slice(h * HALF, (h + 1) * HALF)
+            nc.scalar.activation(shared[:, slots], clamped[:, slots], COPY, scale=both_col[:])
         put(put1[0], lists[0], lam_row, HALF, HALF + PIECE)
         put(put1[1], lists[0], lam_row, HALF + PIECE, I)
-        put(put2, lists[3], both_row, 0, I)
+        nc.vector.tensor_copy(put2[:].indirect(lists[3][:]), shared[:])
 
         partial = [ps.tile([P, BANK], F32, name="partial%d" % b, tag="bank%d" % (4 + b)) for b in range(T // BANK)]
         for n, window in enumerate(put1):

from contextlib import ExitStack

import concourse.mybir as mybir
from concourse.masks import make_identity

D, T, I, Q = 512, 1024, 512, 128
FLOPS = 2 * D * T * Q

F32 = mybir.dt.float32
BF16 = mybir.dt.bfloat16
I32 = mybir.dt.int32
U32 = mybir.dt.uint32
U16 = mybir.dt.uint16
U8 = mybir.dt.uint8
FP8X4 = mybir.dt.float8_e4m3fn_x4
ALU = mybir.AluOpType
COPY = mybir.ActivationFunctionType.Copy

P = 128
PACK = 4
WIDTHS = (256, 256, 256, 128, 128)
HALF = I // 2
PIECE = 128
BANK = 256
STORE = 256
BIG = 2.0 ** 127


def tile_attend_middle_lean_twiceput_heads_kernel(
    tc, query, keys_words, keys_scales, lam, old, share2, offs, offs2, offs3, offs4, out
):
    nc = tc.nc
    with ExitStack() as ctx:
        sb = ctx.enter_context(tc.tile_pool(name="sb", bufs=1))
        ps = ctx.enter_context(tc.psum_pool(name="ps", bufs=1))

        lists = [sb.tile([P, I // 16], U16, name="list%d" % n) for n in range(4)]
        k_scales = sb.tile([P, T], U8, align_bytes=64)
        k_words = [sb.tile([P, T // 2], U32, align_bytes=64, name="k_words%d" % b) for b in range(2)]
        q_raw = sb.tile([P, PACK, Q], F32, align_bytes=64)
        lam_col = sb.tile([P, 1], F32)
        share_col = sb.tile([P, 1], F32)
        old_sb = sb.tile([P, T], F32)

        nc.vector.memset(k_scales[:].bitcast(I32), 0)
        words = keys_words[0].rearrange("p n t -> p (n t)").bitcast(I32)
        nc.sync.dma_start(q_raw[:], query.rearrange("(p j) q -> p j q", j=PACK))
        nc.sync.dma_start(k_words[0][:].bitcast(I32), words[:, : T // 2])
        for quad in range(4):
            nc.sync.dma_start(
                k_scales[32 * quad : 32 * quad + 4, :].bitcast(I32),
                keys_scales[0][4 * quad : 4 * quad + 4, :].bitcast(I32),
            )
        nc.sync.dma_start(k_words[1][:].bitcast(I32), words[:, T // 2 :])
        nc.sync.dma_start(lam_col[:], lam)
        nc.sync.dma_start(lists[0][:], offs)
        nc.sync.dma_start(lists[1][:], offs2)
        nc.sync.dma_start(lists[2][:], offs3)
        nc.sync.dma_start(share_col[:], share2)
        nc.sync.dma_start(lists[3][:], offs4)
        nc.sync.dma_start(old_sb[:], old)

        put1 = [sb.tile([P, T], F32, name="put1_%d" % n) for n in range(2)]
        for window in put1:
            nc.vector.memset(window[:], 0.0)
        ident = sb.tile([P, P], F32)
        make_identity(nc, ident[:])

        q_codes = sb.tile([P, Q], U32, align_bytes=64)
        q_scales = sb.tile([P, Q], U8, align_bytes=64)
        q_halves = [slice(c, c + Q // 2) for c in range(0, Q, Q // 2)]
        q_bf = [sb.tile([P, Q // 2, PACK], BF16, align_bytes=64, name="q_bf%d" % h, tag="q_bf%d" % h) for h in range(2)]
        for h, c in enumerate(q_halves):
            nc.vector.tensor_copy(
                q_bf[h][:].rearrange("p (c i) j -> p c j i", i=4), q_raw[:, :, c].rearrange("p j (c i) -> p c j i", i=4)
            )
        for h, c in enumerate(q_halves):
            nc.vector.quantize_mx(
                q_codes[:, c].bitcast(FP8X4), q_scales[:, c], q_bf[h][:].rearrange("p q j -> p (q j)")
            )

        put2 = sb.tile([P, T], F32, align_bytes=64, tag="q_bf1")
        nc.gpsimd.memset(put2[:], 0.0)

        top = sb.tile([P, 1], F32)
        bottom = sb.tile([P, 1], F32)
        nc.gpsimd.tensor_scalar(top[:], lam_col[:], 0.0, BIG, ALU.is_ge, ALU.mult)
        nc.gpsimd.tensor_scalar(bottom[:], lam_col[:], 0.0, -BIG, ALU.is_lt, ALU.mult)
        lam_row = sb.tile([P, PIECE], F32)
        nc.scalar.activation(lam_row[:], lam_col[:].to_broadcast([P, PIECE]), COPY)

        scores = sb.tile([P, T], F32)
        start = 0
        for n, width in enumerate(WIDTHS):
            cols = slice(start, start + width)
            half, c0 = divmod(start, T // 2)
            acc = ps.tile([P, width], F32, name="acc%d" % n, tag="bank%d" % n)
            nc.tensor.matmul_mx(
                acc[:], q_codes[:].bitcast(FP8X4), q_scales[:], k_words[half][:, c0 : c0 + width].bitcast(FP8X4),
                k_scales[:, cols], start=True, stop=True,
            )
            if n % 2 == 0:
                nc.scalar.copy(scores[:, cols], acc[:])
            else:
                nc.vector.tensor_copy(scores[:, cols], acc[:])
            start = start + width

        turned = [ps.tile([P, BANK], F32, name="turned%d" % b, tag="bank%d" % b) for b in range(T // BANK)]
        for b in range(T // BANK):
            for j in range(BANK // P):
                nc.tensor.matmul(
                    turned[b][:, j * P : (j + 1) * P], old_sb[:, b * BANK + j * P : b * BANK + (j + 1) * P], ident[:],
                    start=(j == 0), stop=False, is_transpose=True,
                )

        clamped = sb.tile([P, I], F32)

        def put(window, offsets, row, start, stop):
            nc.vector.tensor_tensor(
                window[:].indirect(offsets[:, start // 16 : stop // 16]), clamped[:, start:stop], row[:, : stop - start],
                ALU.mult,
            )

        def look_up(h):
            entries = slice(h * HALF // 16, (h + 1) * HALF // 16)
            first = sb.tile([P, HALF], F32, name="first%d" % h)
            second = sb.tile([P, HALF], F32, name="second%d" % h)
            third = sb.tile([P, HALF], F32, name="third%d" % h, tag="third%d" % h)
            nc.scalar.activation(first[:], scores[:].indirect(lists[0][:, entries]), COPY)
            if h == 0:
                nc.vector.tensor_copy(second[:], scores[:].indirect(lists[1][:, entries]))
            else:
                nc.scalar.activation(second[:], scores[:].indirect(lists[1][:, entries]), COPY)
            nc.scalar.activation(third[:], scores[:].indirect(lists[2][:, entries]), COPY)
            pair = sb.tile([P, 2, HALF], F32, name="pair")
            nc.vector.tensor_tensor(pair[:, 0, :], first[:], second[:], ALU.max)
            nc.vector.scalar_tensor_tensor(pair[:, 1, :], first[:], top[:], second[:], ALU.min, ALU.min)
            return pair, third

        mid = sb.tile([P, I], F32)

        def median(h):
            pair, third = look_up(h)
            pieces = [slice(c, c + PIECE) for c in range(0, HALF, PIECE)]
            slots = [slice(h * HALF + c.start, h * HALF + c.stop) for c in pieces]
            for c, d in zip(pieces, slots):
                nc.vector.scalar_tensor_tensor(mid[:, d], pair[:, 0, c], top[:], third[:, c], ALU.min, ALU.min)
            for c, d in zip(pieces, slots):
                nc.vector.scalar_tensor_tensor(clamped[:, d], pair[:, 1, c], bottom[:], mid[:, d], ALU.max, ALU.max)

        median(0)
        put(put1[0], lists[0], lam_row, 0, PIECE)
        put(put1[1], lists[0], lam_row, PIECE, HALF)
        median(1)
        both_col = sb.tile([P, 1], F32)
        nc.gpsimd.tensor_tensor(both_col[:], lam_col[:], share_col[:], ALU.mult)
        shared = sb.tile([P, I], F32)
        for h in range(2):
            slots = slice(h * HALF, (h + 1) * HALF)
            nc.scalar.activation(shared[:, slots], clamped[:, slots], COPY, scale=both_col[:])
        put(put1[0], lists[0], lam_row, HALF, HALF + PIECE)
        put(put1[1], lists[0], lam_row, HALF + PIECE, I)
        nc.vector.tensor_copy(put2[:].indirect(lists[3][:]), shared[:])

        partial = [ps.tile([P, BANK], F32, name="partial%d" % b, tag="bank%d" % (4 + b)) for b in range(T // BANK)]
        for n, window in enumerate(put1):
            for b in range(T // BANK):
                for j in range(BANK // P):
                    nc.tensor.matmul(
                        turned[b][:, j * P : (j + 1) * P], window[:, b * BANK + j * P : b * BANK + (j + 1) * P],
                        ident[:], start=False, stop=(n == 1 and j == BANK // P - 1), is_transpose=True,
                    )
        for b in range(T // BANK):
            turned_sb = sb.tile([P, BANK], F32, name="turned_sb%d" % b)
            nc.scalar.copy(turned_sb[:], turned[b][:])
            for j in range(BANK // P):
                nc.tensor.transpose(partial[b][:, j * P : (j + 1) * P], turned_sb[:, j * P : (j + 1) * P], ident[:])

        for s in range(T // STORE):
            cols = slice(s * STORE, (s + 1) * STORE)
            b, c0 = divmod(s * STORE, BANK)
            total = sb.tile([P, STORE], F32, name="total%d" % s)
            nc.vector.tensor_tensor(total[:], partial[b][:, c0 : c0 + STORE], put2[:, cols], ALU.add)
            (nc.sync if s % 2 == 0 else nc.scalar).dma_start(out[:, cols], total[:])
